import numpy as np
import ml_dtypes


def mxq(x, axis, fmt="e4m3"):
    dtype, down = {"e4m3": (ml_dtypes.float8_e4m3fn, 7), "e5m2": (ml_dtypes.float8_e5m2, 14)}[fmt]
    v = np.moveaxis(np.asarray(x, np.float32).astype(ml_dtypes.bfloat16).astype(np.float64), axis, -1)
    blocks = v.reshape(v.shape[:-1] + (-1, 32))
    amax = np.abs(blocks).max(-1, keepdims=True)
    byte = np.maximum(np.where(amax > 0, np.frexp(amax)[1] - 1 + 127, 0) - down, 1)
    scale = np.exp2(byte - 127.0)
    codes = (blocks / scale).astype(np.float32).astype(dtype).astype(np.float64)
    return np.moveaxis((codes * scale).reshape(v.shape), -1, axis)


WIDE = False


def mx_kscale(k):
    if not WIDE:
        return np.ones(k)
    levels = np.array([10, -10, 5, -5, 0])
    if k % 512:
        return np.exp2(np.random.permutation(np.resize(levels, k // 32))).repeat(32)
    a = np.empty((k // 512, 16))
    for p in range(k // 512):
        a[p, :8] = np.random.permutation(np.resize(levels, 8))
        for g in range(8):
            far = levels[np.abs(levels - a[p, g]) >= 10]
            a[p, g + 8] = far[np.random.randint(len(far))]
    return np.exp2(a.ravel()).repeat(32)


def f64(x):
    return np.asarray(x).astype(np.float64)


def striped(idx):
    return np.tile(idx.reshape(-1, 16).T, (8, 1)).astype(np.uint16)


def unstriped(offs):
    return offs[:16].T.reshape(-1).astype(np.int64)


E2M1 = np.array([0.0, 0.5, 1.0, 1.5, 2.0, 3.0, 4.0, 6.0, -0.0, -0.5, -1.0, -1.5, -2.0, -3.0, -4.0, -6.0])


def pack_weight(w, fmt):
    k, n = w.shape
    w = f64(np.asarray(w, np.float32).astype(ml_dtypes.bfloat16)).reshape(k // 32, 32, n)
    amax = np.abs(w).max(1)
    if fmt == "e4m3":
        byte = np.frexp(amax)[1] - 1 + 127 - 7
    else:
        mant, ex = np.frexp(amax / 6.0)
        byte = np.where(mant > 0.5, ex, ex - 1) + 127
    byte = np.clip(np.where(amax > 0, byte, 1), 1, 254)
    scaled = (w * np.exp2(127.0 - byte)[:, None, :]).reshape(k, n).astype(np.float32)
    by_word = np.ascontiguousarray(scaled.reshape(k // 512, 128, 4, n).transpose(0, 1, 3, 2))
    if fmt == "e4m3":
        words = by_word.astype(ml_dtypes.float8_e4m3fn).view(np.uint8)
    else:
        c = by_word.astype(ml_dtypes.float4_e2m1fn).view(np.uint8) & 0xF
        words = (c[..., 0::2] | (c[..., 1::2] << 4)).reshape(k // 512, 128, 2 * n)
    return np.ascontiguousarray(words), np.ascontiguousarray(byte.astype(np.uint8).reshape(k // 512, 16, n))


def unpack_weight(words, scales, fmt):
    g, _, n = scales.shape
    words = np.ascontiguousarray(words).reshape(g, 128, n, -1)
    if fmt == "e4m3":
        vals = words.view(ml_dtypes.float8_e4m3fn).astype(np.float64)
    else:
        nib = np.empty((g, 128, n, 4), np.uint8)
        nib[..., 0::2] = words & 0xF
        nib[..., 1::2] = words >> 4
        vals = E2M1[nib]
    vals = vals * np.repeat(np.exp2(scales.astype(np.float64) - 127.0), 8, axis=1)[..., None]
    return vals.transpose(0, 1, 3, 2).reshape(g * 512, n)


G, K, M, T, S = 4, 1024, 512, 2048, 256


def setup_inputs():
    n = np.random.standard_normal
    s = mx_kscale(K)[:, None]
    p_w4 = pack_weight(n((K, M)) / np.sqrt(K) / s, "e2m1")
    p_w8 = pack_weight(n((K, M)) / np.sqrt(K) / s, "e4m3")
    return {
        "xT": (n((K, T)) * s).astype(np.float32),
        "c": (n((K, S)) * s).astype(np.float32),
        "w4_words": p_w4[0],
        "w4_scales": p_w4[1],
        "w8_words": p_w8[0],
        "w8_scales": p_w8[1],
        "b": (0.3 * n(512)).astype(np.float32),
        "offs": striped(np.concatenate([np.random.permutation(T)[:S] for _ in range(G)])),
    }


def reference(xT, c, w4_words, w4_scales, w8_words, w8_scales, b, offs):
    idx = unstriped(offs).reshape(G, S)
    xm_ = mxq(np.max([f64(xT)[:, idx[g]] for g in range(G)], axis=0), 0, "e4m3")
    c_ = mxq(f64(c), 0, "e4m3")
    w4_ = unpack_weight(w4_words, w4_scales, "e2m1")
    w8_ = unpack_weight(w8_words, w8_scales, "e4m3")
    y = xm_.T @ w4_ + c_.T @ w8_
    return y + f64(b)[None, :]

@@ -1,0 +1,180 @@
+from contextlib import ExitStack
+
+import concourse.mybir as mybir
+from concourse.masks import make_identity
+
+G, K, M, T, S = 4, 1024, 512, 2048, 256
+FLOPS = 2 * 2 * K * S * M
+
+F32 = mybir.dt.float32
+BF16 = mybir.dt.bfloat16
+I32 = mybir.dt.int32
+U32 = mybir.dt.uint32
+U16 = mybir.dt.uint16
+U8 = mybir.dt.uint8
+E4M3X4 = mybir.dt.float8_e4m3fn_x4
+E2M1X4 = mybir.dt.float4_e2m1fn_x4
+MAX = mybir.AluOpType.max
+ADD = mybir.AluOpType.add
+
+P = 128
+PACK = 4
+PASSES = K // (P * PACK)
+HALVES = S // P
+
+CHUNKS = [(1024, 1024), (1024, 480)]
+LAST_CHUNKS = [(1024, 1024), (512, 0), (512, 176)]
+
+
+def tile_list_sage_tm_bias_kernel(tc, xT, c, w4_words, w4_scales, w8_words, w8_scales, b, offs, out):
+    nc = tc.nc
+    with ExitStack() as ctx:
+        keep = ctx.enter_context(tc.tile_pool(name="keep", bufs=1))
+        psum = ctx.enter_context(tc.psum_pool(name="psum", bufs=1))
+
+        offsets = keep.tile([P, G * S // 16], U16, name="offsets")
+        identity = keep.tile([P, P], F32, name="identity")
+        b_cols = keep.tile([P, PACK], F32, name="b_cols")
+        bias = keep.tile([P, M], F32, name="bias")
+        w4_sc = keep.tile([P, PASSES, M], U8, name="w4_sc", align_bytes=64)
+        w8_sc = keep.tile([P, PASSES, M], U8, name="w8_sc", align_bytes=64)
+        nc.gpsimd.memset(w4_sc[:].bitcast(I32), 0)
+        nc.gpsimd.memset(w8_sc[:].bitcast(I32), 0)
+        make_identity(nc, identity[:])
+
+        def load_scale_rows(plane, src, q):
+            nc.sync.dma_start(
+                out=plane[32 * q : 32 * q + 4, :, :].bitcast(I32),
+                in_=src[:, 4 * q : 4 * q + 4, :].rearrange("a r n -> r a n").bitcast(I32),
+            )
+
+        small = [
+            lambda: nc.sync.dma_start(offsets[:], offs),
+            lambda: nc.sync.dma_start(out=b_cols[:], in_=b.rearrange("(p i) -> p i", i=PACK)),
+        ]
+        for q in range(4):
+            small.append(lambda q=q: load_scale_rows(w4_sc, w4_scales, q))
+        for q in range(4):
+            small.append(lambda q=q: load_scale_rows(w8_sc, w8_scales, q))
+
+        x_planes = xT.rearrange("(a p i) t -> a p i t", a=PASSES, i=PACK)
+        pairs = [(a, u) for a in range(PASSES) for u in range(2)]
+        raws = {}
+        n_loads = 0
+        for a, u in pairs:
+            t0 = 0
+            chunks = LAST_CHUNKS if (a, u) == pairs[-1] else CHUNKS
+            for n, (width, on_scalar) in enumerate(chunks):
+                raw = keep.tile([P, 2, width], F32, name="raw%d%d%d" % (a, u, n))
+                nc.sync.dma_start(out=raw[:], in_=x_planes[a][:, 2 * u : 2 * u + 2, t0 : t0 + width])
+                raws.setdefault((a, u), []).append((raw, t0, width, on_scalar))
+                t0 = t0 + width
+                n_loads = n_loads + 1
+                if 2 <= n_loads <= 6:
+                    small[2 * (n_loads - 2)]()
+                    small[2 * (n_loads - 2) + 1]()
+
+        c_planes = c.rearrange("(a p i) j -> a p i j", a=PASSES, i=PACK)
+        c_raw = [keep.tile([P, PACK, S], F32, name="c_raw%d" % a) for a in range(PASSES)]
+        w4 = [keep.tile([P, 2 * M], U8, name="w4_%d" % a, align_bytes=64) for a in range(PASSES)]
+        w8 = [keep.tile([P, 4 * M], U8, name="w8_%d" % a, align_bytes=64) for a in range(PASSES)]
+
+        def load_w4(a):
+            nc.sync.dma_start(out=w4[a][:].bitcast(I32), in_=w4_words[a].bitcast(I32))
+
+        def load_w8(a):
+            nc.sync.dma_start(out=w8[a][:].bitcast(I32), in_=w8_words[a].rearrange("p n i -> p (n i)").bitcast(I32))
+
+        nc.sync.dma_start(out=c_raw[0][:], in_=c_planes[0])
+        load_w4(0)
+        nc.sync.dma_start(out=c_raw[1][:], in_=c_planes[1])
+        load_w8(0)
+        load_w8(1)
+        load_w4(1)
+
+        b_ps = psum.tile([P, PACK, P], F32, name="b_ps")
+        for i in range(PACK):
+            nc.tensor.transpose(b_ps[:, i, :], b_cols[:, i : i + 1].to_broadcast([P, P]), identity[:])
+        nc.scalar.copy(out=bias[:].rearrange("p (q i) -> p q i", i=PACK), in_=b_ps[:].rearrange("p i q -> p q i"))
+
+        def quantize(grouped, name):
+            codes = keep.tile([P, P], U32, name=name + "_codes", align_bytes=64)
+            scales = keep.tile([P, P], U8, name=name + "_scales", align_bytes=64)
+            nc.vector.quantize_mx(out=codes[:].bitcast(E4M3X4), scales=scales[:], in_=grouped[:])
+            return codes, scales
+
+        def cast_c(a, h):
+            grouped = keep.tile([P, P * PACK], BF16, name="c_grouped%d%d" % (a, h), align_bytes=64)
+            nc.scalar.copy(
+                out=grouped[:].rearrange("p (r s i) -> p r i s", s=4, i=PACK),
+                in_=c_raw[a][:, :, h * P : (h + 1) * P].rearrange("p i (r s) -> p r i s", s=4),
+            )
+            return grouped
+
+        def gather_pair(a, u):
+            window = keep.tile([P, T * 2], BF16, name="window%d%d" % (a, u))
+            woven = window[:].rearrange("p (t e) -> p t e", e=2)
+            for raw, t0, width, on_scalar in raws[(a, u)]:
+                src = raw[:].rearrange("p e t -> p t e")
+                if on_scalar > 0:
+                    nc.scalar.copy(out=woven[:, t0 : t0 + on_scalar, :], in_=src[:, 0:on_scalar, :])
+                if on_scalar < width:
+                    nc.vector.tensor_copy(out=woven[:, t0 + on_scalar : t0 + width, :], in_=src[:, on_scalar:width, :])
+            picked = keep.tile([P, G * S], U32, name="picked%d%d" % (a, u))
+            nc.vector.tensor_copy(picked[:], window[:].bitcast(U32).indirect(offsets[:]))
+            return picked
+
+        def max_pair(picked, maxima, a, u, parts):
+            by_g = picked[:].bitcast(BF16).rearrange("p (g w) -> p g w", g=G)
+            two = keep.tile([P, 2, 2 * S], BF16, name="two%d%d" % (a, u))
+            width = 2 * S // parts
+            spans = [slice(n * width, (n + 1) * width) for n in range(parts)]
+            for span in spans:
+                nc.vector.tensor_tensor(two[:, :, span], by_g[:, 0:2, span], by_g[:, 2:4, span], MAX)
+            for span in spans:
+                nc.vector.tensor_tensor(maxima[:, u, span], two[:, 0, span], two[:, 1, span], MAX)
+
+        def weave(maxima, a, copy, word):
+            grouped = [keep.tile([P, P * PACK], BF16, name="x_grouped%d%d" % (a, h), align_bytes=64) for h in range(HALVES)]
+            words = maxima[:].bitcast(word).rearrange("p u j -> p j u")
+            for h in range(HALVES):
+                copy(out=grouped[h][:].bitcast(word).rearrange("p (j u) -> p j u", u=2), in_=words[:, h * P : (h + 1) * P, :])
+            return grouped
+
+        acc = [psum.tile([P, M], F32, name="acc%d" % h) for h in range(HALVES)]
+
+        def multiply(h, operand, weight, weight_scales, a, start=False, stop=False):
+            nc.tensor.matmul_mx(
+                out=acc[h][:],
+                lhsT=operand[0][:].bitcast(E4M3X4),
+                lhsT_scale=operand[1][:],
+                rhs=weight,
+                rhs_scale=weight_scales[:, a, :],
+                start=start,
+                stop=stop,
+            )
+
+        maxima = [keep.tile([P, 2, 2 * S], BF16, name="maxima%d" % a) for a in range(PASSES)]
+        for u in range(2):
+            max_pair(gather_pair(0, u), maxima[0], 0, u, 1)
+        grouped = weave(maxima[0], 0, nc.scalar.copy, U32)
+        picked = gather_pair(1, 0)
+        xm0 = [quantize(grouped[h], "xm0%d" % h) for h in range(HALVES)]
+        max_pair(picked, maxima[1], 1, 0, 1)
+        picked = gather_pair(1, 1)
+        c0 = [quantize(cast_c(0, h), "c0%d" % h) for h in range(HALVES)]
+        max_pair(picked, maxima[1], 1, 1, HALVES)
+        c1 = [quantize(cast_c(1, h), "c1%d" % h) for h in range(HALVES)]
+        grouped = weave(maxima[1], 1, nc.vector.tensor_copy, I32)
+        xm1 = [quantize(grouped[h], "xm1%d" % h) for h in range(HALVES)]
+
+        for h in range(HALVES):
+            multiply(h, xm0[h], w4[0][:].bitcast(E2M1X4), w4_sc, 0, start=True)
+        for a, operand in enumerate([c0, c1]):
+            for h in range(HALVES):
+                multiply(h, operand[h], w8[a][:].bitcast(E4M3X4), w8_sc, a)
+        for h in range(HALVES):
+            multiply(h, xm1[h], w4[1][:].bitcast(E2M1X4), w4_sc, 1, stop=True)
+            result = keep.tile([P, M], F32, name="result%d" % h)
+            nc.vector.tensor_tensor(result[:], acc[h][:], bias[:], ADD)
+            nc.sync.dma_start(out=out[h * P : (h + 1) * P, :], in_=result[:])

@@ -22,8 +22,12 @@ PACK = 4
 PASSES = K // (P * PACK)
 HALVES = S // P
 
-CHUNKS = [(1024, 1024), (1024, 480)]
-LAST_CHUNKS = [(1024, 1024), (512, 0), (512, 176)]
+CHUNKS = [
+    [(1024, 352), (1024, 352)],
+    [(1024, 1024), (1024, 352)],
+    [(1024, 1024), (1024, 352)],
+    [(1024, 1024), (1024, 384)],
+]
 
 
 def tile_list_sage_tm_bias_kernel(tc, xT, c, w4_words, w4_scales, w8_words, w8_scales, b, offs, out):
@@ -48,14 +52,7 @@ def tile_list_sage_tm_bias_kernel(tc, xT, c, w4_words, w4_scales, w8_words, w8_s
                 in_=src[:, 4 * q : 4 * q + 4, :].rearrange("a r n -> r a n").bitcast(I32),
             )
 
-        small = [
-            lambda: nc.sync.dma_start(offsets[:], offs),
-            lambda: nc.sync.dma_start(out=b_cols[:], in_=b.rearrange("(p i) -> p i", i=PACK)),
-        ]
-        for q in range(4):
-            small.append(lambda q=q: load_scale_rows(w4_sc, w4_scales, q))
-        for q in range(4):
-            small.append(lambda q=q: load_scale_rows(w8_sc, w8_scales, q))
+        nc.scalar.dma_start(out=b_cols[:], in_=b.rearrange("(p i) -> p i", i=PACK))
 
         x_planes = xT.rearrange("(a p i) t -> a p i t", a=PASSES, i=PACK)
         pairs = [(a, u) for a in range(PASSES) for u in range(2)]
@@ -63,19 +60,18 @@ def tile_list_sage_tm_bias_kernel(tc, xT, c, w4_words, w4_scales, w8_words, w8_s
         n_loads = 0
         for a, u in pairs:
             t0 = 0
-            chunks = LAST_CHUNKS if (a, u) == pairs[-1] else CHUNKS
+            chunks = CHUNKS[2 * a + u]
             for n, (width, on_scalar) in enumerate(chunks):
-                raw = keep.tile([P, 2, width], F32, name="raw%d%d%d" % (a, u, n))
+                raw = keep.tile([P, 2, width], F32, name="raw%d%d%d" % (a, u, n), align_bytes=64)
                 nc.sync.dma_start(out=raw[:], in_=x_planes[a][:, 2 * u : 2 * u + 2, t0 : t0 + width])
                 raws.setdefault((a, u), []).append((raw, t0, width, on_scalar))
                 t0 = t0 + width
                 n_loads = n_loads + 1
-                if 2 <= n_loads <= 6:
-                    small[2 * (n_loads - 2)]()
-                    small[2 * (n_loads - 2) + 1]()
+                if n_loads == 1:
+                    nc.sync.dma_start(offsets[:], offs)
 
         c_planes = c.rearrange("(a p i) j -> a p i j", a=PASSES, i=PACK)
-        c_raw = [keep.tile([P, PACK, S], F32, name="c_raw%d" % a) for a in range(PASSES)]
+        c_raw = [keep.tile([P, PACK, S], F32, name="c_raw%d" % a, align_bytes=64) for a in range(PASSES)]
         w4 = [keep.tile([P, 2 * M], U8, name="w4_%d" % a, align_bytes=64) for a in range(PASSES)]
         w8 = [keep.tile([P, 4 * M], U8, name="w8_%d" % a, align_bytes=64) for a in range(PASSES)]
 
@@ -86,8 +82,12 @@ def tile_list_sage_tm_bias_kernel(tc, xT, c, w4_words, w4_scales, w8_words, w8_s
             nc.sync.dma_start(out=w8[a][:].bitcast(I32), in_=w8_words[a].rearrange("p n i -> p (n i)").bitcast(I32))
 
         nc.sync.dma_start(out=c_raw[0][:], in_=c_planes[0])
+        for q in range(4):
+            load_scale_rows(w4_sc, w4_scales, q)
         load_w4(0)
         nc.sync.dma_start(out=c_raw[1][:], in_=c_planes[1])
+        for q in range(4):
+            load_scale_rows(w8_sc, w8_scales, q)
         load_w8(0)
         load_w8(1)
         load_w4(1)
@@ -100,16 +100,16 @@ def tile_list_sage_tm_bias_kernel(tc, xT, c, w4_words, w4_scales, w8_words, w8_s
         def quantize(grouped, name):
             codes = keep.tile([P, P], U32, name=name + "_codes", align_bytes=64)
             scales = keep.tile([P, P], U8, name=name + "_scales", align_bytes=64)
-            nc.vector.quantize_mx(out=codes[:].bitcast(E4M3X4), scales=scales[:], in_=grouped[:])
+            nc.vector.quantize_mx(out=codes[:].bitcast(E4M3X4), scales=scales[:], in_=grouped)
             return codes, scales
 
-        def cast_c(a, h):
-            grouped = keep.tile([P, P * PACK], BF16, name="c_grouped%d%d" % (a, h), align_bytes=64)
+        def cast_c(a):
+            grouped = keep.tile([P, S * PACK], BF16, name="c_grouped%d" % a, align_bytes=64)
             nc.scalar.copy(
                 out=grouped[:].rearrange("p (r s i) -> p r i s", s=4, i=PACK),
-                in_=c_raw[a][:, :, h * P : (h + 1) * P].rearrange("p i (r s) -> p r i s", s=4),
+                in_=c_raw[a][:].rearrange("p i (r s) -> p r i s", s=4),
             )
-            return grouped
+            return [grouped[:, h * P * PACK : (h + 1) * P * PACK] for h in range(HALVES)]
 
         def gather_pair(a, u):
             window = keep.tile([P, T * 2], BF16, name="window%d%d" % (a, u))
@@ -120,26 +120,32 @@ def tile_list_sage_tm_bias_kernel(tc, xT, c, w4_words, w4_scales, w8_words, w8_s
                     nc.scalar.copy(out=woven[:, t0 : t0 + on_scalar, :], in_=src[:, 0:on_scalar, :])
                 if on_scalar < width:
                     nc.vector.tensor_copy(out=woven[:, t0 + on_scalar : t0 + width, :], in_=src[:, on_scalar:width, :])
-            picked = keep.tile([P, G * S], U32, name="picked%d%d" % (a, u))
-            nc.vector.tensor_copy(picked[:], window[:].bitcast(U32).indirect(offsets[:]))
+            picked = [keep.tile([P, 2 * S], U32, name="picked%d%d%d" % (a, u, n)) for n in range(2)]
+            for n in range(2):
+                nc.vector.tensor_copy(picked[n][:], window[:].bitcast(U32).indirect(offsets[:, 32 * n : 32 * n + 32]))
             return picked
 
-        def max_pair(picked, maxima, a, u, parts):
-            by_g = picked[:].bitcast(BF16).rearrange("p (g w) -> p g w", g=G)
-            two = keep.tile([P, 2, 2 * S], BF16, name="two%d%d" % (a, u))
-            width = 2 * S // parts
-            spans = [slice(n * width, (n + 1) * width) for n in range(parts)]
-            for span in spans:
-                nc.vector.tensor_tensor(two[:, :, span], by_g[:, 0:2, span], by_g[:, 2:4, span], MAX)
-            for span in spans:
-                nc.vector.tensor_tensor(maxima[:, u, span], two[:, 0, span], two[:, 1, span], MAX)
-
-        def weave(maxima, a, copy, word):
-            grouped = [keep.tile([P, P * PACK], BF16, name="x_grouped%d%d" % (a, h), align_bytes=64) for h in range(HALVES)]
-            words = maxima[:].bitcast(word).rearrange("p u j -> p j u")
+        def max_pair(picked, maxima, u, spaces):
+            two = [space.rearrange("p (n w) -> p n w", n=2) for space in spaces]
+            for n in range(2):
+                by_g = picked[n][:].bitcast(BF16).rearrange("p (g h w) -> p g h w", g=2, h=HALVES)
+                for h in range(HALVES):
+                    nc.vector.tensor_tensor(two[h][:, n, :], by_g[:, 0, h, :], by_g[:, 1, h, :], MAX)
             for h in range(HALVES):
-                copy(out=grouped[h][:].bitcast(word).rearrange("p (j u) -> p j u", u=2), in_=words[:, h * P : (h + 1) * P, :])
-            return grouped
+                nc.vector.tensor_tensor(maxima[h][:, u * 2 * P : (u + 1) * 2 * P], two[h][:, 0, :], two[h][:, 1, :], MAX)
+
+        def fresh(name):
+            return [keep.tile([P, 4 * P], BF16, name="%s%d" % (name, h))[:] for h in range(HALVES)]
+
+        def weave(maxima, tag):
+            grouped = keep.tile([P, S * PACK], BF16, name=tag, align_bytes=64)
+            halves = [grouped[:, h * P * PACK : (h + 1) * P * PACK] for h in range(HALVES)]
+            for h in range(HALVES):
+                nc.scalar.copy(
+                    out=halves[h].bitcast(U32).rearrange("p (j u) -> p j u", u=2),
+                    in_=maxima[h][:].bitcast(U32).rearrange("p (u j) -> p j u", u=2),
+                )
+            return halves
 
         acc = [psum.tile([P, M], F32, name="acc%d" % h) for h in range(HALVES)]
 
@@ -154,18 +160,19 @@ def tile_list_sage_tm_bias_kernel(tc, xT, c, w4_words, w4_scales, w8_words, w8_s
                 stop=stop,
             )
 
-        maxima = [keep.tile([P, 2, 2 * S], BF16, name="maxima%d" % a) for a in range(PASSES)]
+        maxima = [[keep.tile([P, 4 * P], BF16, name="maxima%d%d" % (a, h)) for h in range(HALVES)] for a in range(PASSES)]
         for u in range(2):
-            max_pair(gather_pair(0, u), maxima[0], 0, u, 1)
-        grouped = weave(maxima[0], 0, nc.scalar.copy, U32)
+            max_pair(gather_pair(0, u), maxima[0], u, fresh("two0%d" % u))
         picked = gather_pair(1, 0)
+        grouped = weave(maxima[0], "raw101")
         xm0 = [quantize(grouped[h], "xm0%d" % h) for h in range(HALVES)]
-        max_pair(picked, maxima[1], 1, 0, 1)
+        max_pair(picked, maxima[1], 0, fresh("two10"))
         picked = gather_pair(1, 1)
-        c0 = [quantize(cast_c(0, h), "c0%d" % h) for h in range(HALVES)]
-        max_pair(picked, maxima[1], 1, 1, HALVES)
-        c1 = [quantize(cast_c(1, h), "c1%d" % h) for h in range(HALVES)]
-        grouped = weave(maxima[1], 1, nc.vector.tensor_copy, I32)
+        c_grouped = [cast_c(a) for a in range(PASSES)]
+        c0 = [quantize(c_grouped[0][h], "c0%d" % h) for h in range(HALVES)]
+        max_pair(picked, maxima[1], 1, c_grouped[0])
+        c1 = [quantize(c_grouped[1][h], "c1%d" % h) for h in range(HALVES)]
+        grouped = weave(maxima[1], "c_raw1")
         xm1 = [quantize(grouped[h], "xm1%d" % h) for h in range(HALVES)]
 
         for h in range(HALVES):
@@ -175,6 +182,9 @@ def tile_list_sage_tm_bias_kernel(tc, xT, c, w4_words, w4_scales, w8_words, w8_s
                 multiply(h, operand[h], w8[a][:].bitcast(E4M3X4), w8_sc, a)
         for h in range(HALVES):
             multiply(h, xm1[h], w4[1][:].bitcast(E2M1X4), w4_sc, 1, stop=True)
-            result = keep.tile([P, M], F32, name="result%d" % h)
-            nc.vector.tensor_tensor(result[:], acc[h][:], bias[:], ADD)
-            nc.sync.dma_start(out=out[h * P : (h + 1) * P, :], in_=result[:])
+            parts = h + 1
+            for n in range(parts):
+                cols = slice(n * M // parts, (n + 1) * M // parts)
+                result = keep.tile([P, M // parts], F32, name="result%d%d" % (h, n))
+                nc.vector.tensor_tensor(result[:], acc[h][:, cols], bias[:, cols], ADD)
+                nc.sync.dma_start(out=out[h * P : (h + 1) * P, cols], in_=result[:])

from contextlib import ExitStack

import concourse.mybir as mybir
from concourse.masks import make_identity

G, K, M, T, S = 4, 1024, 512, 2048, 256
FLOPS = 2 * 2 * K * S * M

F32 = mybir.dt.float32
BF16 = mybir.dt.bfloat16
I32 = mybir.dt.int32
U32 = mybir.dt.uint32
U16 = mybir.dt.uint16
U8 = mybir.dt.uint8
E4M3X4 = mybir.dt.float8_e4m3fn_x4
E2M1X4 = mybir.dt.float4_e2m1fn_x4
MAX = mybir.AluOpType.max
ADD = mybir.AluOpType.add

P = 128
PACK = 4
PASSES = K // (P * PACK)
HALVES = S // P

CHUNKS = [
    [(1024, 352), (1024, 352)],
    [(1024, 1024), (1024, 352)],
    [(1024, 1024), (1024, 352)],
    [(1024, 1024), (1024, 384)],
]


def tile_list_sage_tm_bias_kernel(tc, xT, c, w4_words, w4_scales, w8_words, w8_scales, b, offs, out):
    nc = tc.nc
    with ExitStack() as ctx:
        keep = ctx.enter_context(tc.tile_pool(name="keep", bufs=1))
        psum = ctx.enter_context(tc.psum_pool(name="psum", bufs=1))

        offsets = keep.tile([P, G * S // 16], U16, name="offsets")
        identity = keep.tile([P, P], F32, name="identity")
        b_cols = keep.tile([P, PACK], F32, name="b_cols")
        bias = keep.tile([P, M], F32, name="bias")
        w4_sc = keep.tile([P, PASSES, M], U8, name="w4_sc", align_bytes=64)
        w8_sc = keep.tile([P, PASSES, M], U8, name="w8_sc", align_bytes=64)
        nc.gpsimd.memset(w4_sc[:].bitcast(I32), 0)
        nc.gpsimd.memset(w8_sc[:].bitcast(I32), 0)
        make_identity(nc, identity[:])

        def load_scale_rows(plane, src, q):
            nc.sync.dma_start(
                out=plane[32 * q : 32 * q + 4, :, :].bitcast(I32),
                in_=src[:, 4 * q : 4 * q + 4, :].rearrange("a r n -> r a n").bitcast(I32),
            )

        nc.scalar.dma_start(out=b_cols[:], in_=b.rearrange("(p i) -> p i", i=PACK))

        x_planes = xT.rearrange("(a p i) t -> a p i t", a=PASSES, i=PACK)
        pairs = [(a, u) for a in range(PASSES) for u in range(2)]
        raws = {}
        n_loads = 0
        for a, u in pairs:
            t0 = 0
            chunks = CHUNKS[2 * a + u]
            for n, (width, on_scalar) in enumerate(chunks):
                raw = keep.tile([P, 2, width], F32, name="raw%d%d%d" % (a, u, n), align_bytes=64)
                nc.sync.dma_start(out=raw[:], in_=x_planes[a][:, 2 * u : 2 * u + 2, t0 : t0 + width])
                raws.setdefault((a, u), []).append((raw, t0, width, on_scalar))
                t0 = t0 + width
                n_loads = n_loads + 1
                if n_loads == 1:
                    nc.sync.dma_start(offsets[:], offs)

        c_planes = c.rearrange("(a p i) j -> a p i j", a=PASSES, i=PACK)
        c_raw = [keep.tile([P, PACK, S], F32, name="c_raw%d" % a, align_bytes=64) for a in range(PASSES)]
        w4 = [keep.tile([P, 2 * M], U8, name="w4_%d" % a, align_bytes=64) for a in range(PASSES)]
        w8 = [keep.tile([P, 4 * M], U8, name="w8_%d" % a, align_bytes=64) for a in range(PASSES)]

        def load_w4(a):
            nc.sync.dma_start(out=w4[a][:].bitcast(I32), in_=w4_words[a].bitcast(I32))

        def load_w8(a):
            nc.sync.dma_start(out=w8[a][:].bitcast(I32), in_=w8_words[a].rearrange("p n i -> p (n i)").bitcast(I32))

        nc.sync.dma_start(out=c_raw[0][:], in_=c_planes[0])
        for q in range(4):
            load_scale_rows(w4_sc, w4_scales, q)
        load_w4(0)
        nc.sync.dma_start(out=c_raw[1][:], in_=c_planes[1])
        for q in range(4):
            load_scale_rows(w8_sc, w8_scales, q)
        load_w8(0)
        load_w8(1)
        load_w4(1)

        b_ps = psum.tile([P, PACK, P], F32, name="b_ps")
        for i in range(PACK):
            nc.tensor.transpose(b_ps[:, i, :], b_cols[:, i : i + 1].to_broadcast([P, P]), identity[:])
        nc.scalar.copy(out=bias[:].rearrange("p (q i) -> p q i", i=PACK), in_=b_ps[:].rearrange("p i q -> p q i"))

        def quantize(grouped, name):
            codes = keep.tile([P, P], U32, name=name + "_codes", align_bytes=64)
            scales = keep.tile([P, P], U8, name=name + "_scales", align_bytes=64)
            nc.vector.quantize_mx(out=codes[:].bitcast(E4M3X4), scales=scales[:], in_=grouped)
            return codes, scales

        def cast_c(a):
            grouped = keep.tile([P, S * PACK], BF16, name="c_grouped%d" % a, align_bytes=64)
            nc.scalar.copy(
                out=grouped[:].rearrange("p (r s i) -> p r i s", s=4, i=PACK),
                in_=c_raw[a][:].rearrange("p i (r s) -> p r i s", s=4),
            )
            return [grouped[:, h * P * PACK : (h + 1) * P * PACK] for h in range(HALVES)]

        def gather_pair(a, u):
            window = keep.tile([P, T * 2], BF16, name="window%d%d" % (a, u))
            woven = window[:].rearrange("p (t e) -> p t e", e=2)
            for raw, t0, width, on_scalar in raws[(a, u)]:
                src = raw[:].rearrange("p e t -> p t e")
                if on_scalar > 0:
                    nc.scalar.copy(out=woven[:, t0 : t0 + on_scalar, :], in_=src[:, 0:on_scalar, :])
                if on_scalar < width:
                    nc.vector.tensor_copy(out=woven[:, t0 + on_scalar : t0 + width, :], in_=src[:, on_scalar:width, :])
            picked = [keep.tile([P, 2 * S], U32, name="picked%d%d%d" % (a, u, n)) for n in range(2)]
            for n in range(2):
                nc.vector.tensor_copy(picked[n][:], window[:].bitcast(U32).indirect(offsets[:, 32 * n : 32 * n + 32]))
            return picked

        def max_pair(picked, maxima, u, spaces):
            two = [space.rearrange("p (n w) -> p n w", n=2) for space in spaces]
            for n in range(2):
                by_g = picked[n][:].bitcast(BF16).rearrange("p (g h w) -> p g h w", g=2, h=HALVES)
                for h in range(HALVES):
                    nc.vector.tensor_tensor(two[h][:, n, :], by_g[:, 0, h, :], by_g[:, 1, h, :], MAX)
            for h in range(HALVES):
                nc.vector.tensor_tensor(maxima[h][:, u * 2 * P : (u + 1) * 2 * P], two[h][:, 0, :], two[h][:, 1, :], MAX)

        def fresh(name):
            return [keep.tile([P, 4 * P], BF16, name="%s%d" % (name, h))[:] for h in range(HALVES)]

        def weave(maxima, tag):
            grouped = keep.tile([P, S * PACK], BF16, name=tag, align_bytes=64)
            halves = [grouped[:, h * P * PACK : (h + 1) * P * PACK] for h in range(HALVES)]
            for h in range(HALVES):
                nc.scalar.copy(
                    out=halves[h].bitcast(U32).rearrange("p (j u) -> p j u", u=2),
                    in_=maxima[h][:].bitcast(U32).rearrange("p (u j) -> p j u", u=2),
                )
            return halves

        acc = [psum.tile([P, M], F32, name="acc%d" % h) for h in range(HALVES)]

        def multiply(h, operand, weight, weight_scales, a, start=False, stop=False):
            nc.tensor.matmul_mx(
                out=acc[h][:],
                lhsT=operand[0][:].bitcast(E4M3X4),
                lhsT_scale=operand[1][:],
                rhs=weight,
                rhs_scale=weight_scales[:, a, :],
                start=start,
                stop=stop,
            )

        maxima = [[keep.tile([P, 4 * P], BF16, name="maxima%d%d" % (a, h)) for h in range(HALVES)] for a in range(PASSES)]
        for u in range(2):
            max_pair(gather_pair(0, u), maxima[0], u, fresh("two0%d" % u))
        picked = gather_pair(1, 0)
        grouped = weave(maxima[0], "raw101")
        xm0 = [quantize(grouped[h], "xm0%d" % h) for h in range(HALVES)]
        max_pair(picked, maxima[1], 0, fresh("two10"))
        picked = gather_pair(1, 1)
        c_grouped = [cast_c(a) for a in range(PASSES)]
        c0 = [quantize(c_grouped[0][h], "c0%d" % h) for h in range(HALVES)]
        max_pair(picked, maxima[1], 1, c_grouped[0])
        c1 = [quantize(c_grouped[1][h], "c1%d" % h) for h in range(HALVES)]
        grouped = weave(maxima[1], "c_raw1")
        xm1 = [quantize(grouped[h], "xm1%d" % h) for h in range(HALVES)]

        for h in range(HALVES):
            multiply(h, xm0[h], w4[0][:].bitcast(E2M1X4), w4_sc, 0, start=True)
        for a, operand in enumerate([c0, c1]):
            for h in range(HALVES):
                multiply(h, operand[h], w8[a][:].bitcast(E4M3X4), w8_sc, a)
        for h in range(HALVES):
            multiply(h, xm1[h], w4[1][:].bitcast(E2M1X4), w4_sc, 1, stop=True)
            parts = h + 1
            for n in range(parts):
                cols = slice(n * M // parts, (n + 1) * M // parts)
                result = keep.tile([P, M // parts], F32, name="result%d%d" % (h, n))
                nc.vector.tensor_tensor(result[:], acc[h][:, cols], bias[:, cols], ADD)
                nc.sync.dma_start(out=out[h * P : (h + 1) * P, cols], in_=result[:])
